import numpy as np
import ml_dtypes


def mxq(x, axis, fmt="e4m3"):
    dtype, down = {"e4m3": (ml_dtypes.float8_e4m3fn, 7), "e5m2": (ml_dtypes.float8_e5m2, 14)}[fmt]
    v = np.moveaxis(np.asarray(x, np.float32).astype(ml_dtypes.bfloat16).astype(np.float64), axis, -1)
    blocks = v.reshape(v.shape[:-1] + (-1, 32))
    amax = np.abs(blocks).max(-1, keepdims=True)
    byte = np.maximum(np.where(amax > 0, np.frexp(amax)[1] - 1 + 127, 0) - down, 1)
    scale = np.exp2(byte - 127.0)
    codes = (blocks / scale).astype(np.float32).astype(dtype).astype(np.float64)
    return np.moveaxis((codes * scale).reshape(v.shape), -1, axis)


WIDE = False


def mx_kscale(k):
    if not WIDE:
        return np.ones(k)
    levels = np.array([10, -10, 5, -5, 0])
    if k % 512:
        return np.exp2(np.random.permutation(np.resize(levels, k // 32))).repeat(32)
    a = np.empty((k // 512, 16))
    for p in range(k // 512):
        a[p, :8] = np.random.permutation(np.resize(levels, 8))
        for g in range(8):
            far = levels[np.abs(levels - a[p, g]) >= 10]
            a[p, g + 8] = far[np.random.randint(len(far))]
    return np.exp2(a.ravel()).repeat(32)


def f64(x):
    return np.asarray(x).astype(np.float64)


def striped(idx):
    return np.tile(idx.reshape(-1, 16).T, (8, 1)).astype(np.uint16)


def unstriped(offs):
    return offs[:16].T.reshape(-1).astype(np.int64)


def striped8(idx):
    return np.concatenate([x.reshape(-1, 16).T for x in idx]).astype(np.uint16)


def runs(offs, k):
    lists = np.stack([offs[16 * r : 16 * r + 16].T.reshape(-1) for r in range(8)]).astype(np.int64)
    return lists[np.arange(k) % 512 // 64]


def pack_weight(w):
    k, n = w.shape
    w = f64(np.asarray(w, np.float32).astype(ml_dtypes.bfloat16)).reshape(k // 32, 32, n)
    amax = np.abs(w).max(1)
    byte = np.clip(np.where(amax > 0, np.frexp(amax)[1] - 1 + 127 - 7, 1), 1, 254)
    scaled = (w * np.exp2(127.0 - byte)[:, None, :]).reshape(k, n).astype(np.float32)
    words = np.ascontiguousarray(scaled.reshape(k // 512, 128, 4, n).transpose(0, 1, 3, 2)).astype(ml_dtypes.float8_e4m3fn).view(np.uint8)
    return words, np.ascontiguousarray(byte.astype(np.uint8).reshape(k // 512, 16, n))


def unpack_weight(words, scales):
    g, p, n, _ = words.shape
    vals = np.ascontiguousarray(words).view(ml_dtypes.float8_e4m3fn).astype(np.float64) * np.repeat(np.exp2(scales.astype(np.float64) - 127.0), 8, axis=1)[..., None]
    return vals.transpose(0, 1, 3, 2).reshape(g * 512, n)

def planes(y):
    n, m = y.shape
    v = y.astype(np.float32).astype(ml_dtypes.bfloat16).astype(np.float64).reshape(n // 32, 32, m)
    top = np.abs(v).max(1)
    byte = np.clip(np.where(top > 0, np.frexp(top)[1] - 1 + 127 - 7, 1), 1, 254)
    codes = (v * np.exp2(127.0 - byte)[:, None, :]).reshape(n, m).astype(np.float32).astype(ml_dtypes.float8_e4m3fn).view(np.uint8)
    words = codes.reshape(n // 512, 128, 4, m).transpose(0, 1, 3, 2)
    return np.ascontiguousarray(words), np.ascontiguousarray(byte.astype(np.uint8).reshape(n // 512, 16, m))


K, T, S, H, J = 512, 2048, 512, 512, 512


def setup_inputs():
    n = np.random.standard_normal
    s = mx_kscale(K)[:, None]
    u = mx_kscale(H)
    packed_xT = pack_weight(n((K, T)) * s)
    packed_w1 = pack_weight(n((K, H)) / np.sqrt(K) / s)
    packed_w2 = pack_weight(n((H, H)) / np.sqrt(H) / u[:, None])
    return {
        "x_words": packed_xT[0],
        "x_scales": packed_xT[1],
        "w1_words": packed_w1[0],
        "w1_scales": packed_w1[1],
        "tab": n((H, J)).astype(np.float32),
        "tab2": np.random.uniform(0.4, 1.4, (H, J)).astype(np.float32),
        "gn": (np.random.uniform(0.5, 1.5, (H, 1)) * u[:, None]).astype(np.float32),
        "w2_words": packed_w2[0],
        "w2_scales": packed_w2[1],
        "offs": striped(np.random.permutation(T)[:S]),
        "n1": striped8(np.random.randint(0, J, (8, S))),
        "n2": striped8(np.stack([np.random.permutation(S) for _ in range(8)])),
        "n3": striped8(np.random.randint(0, J, (8, S))),
        "n4": striped8(np.stack([np.random.permutation(S) for _ in range(8)])),
        "n5": striped8(np.stack([np.random.permutation(S) for _ in range(8)])),
        "n6": striped8(np.stack([np.random.permutation(S) for _ in range(8)])),
        "n7": striped8(np.stack([np.random.permutation(S) for _ in range(8)])),
        "n8": striped8(np.stack([np.random.permutation(S) for _ in range(8)])),
    }


def reference(x_words, x_scales, w1_words, w1_scales, tab, tab2, gn, w2_words, w2_scales, offs, n1, n2, n3, n4, n5, n6, n7, n8):
    xq = unpack_weight(x_words, x_scales)[:, unstriped(offs)]
    y = unpack_weight(w1_words, w1_scales).T @ xq
    z = f64(gn) * (np.abs(y - (y[np.arange(H)[:, None], runs(n2, H)]) - (f64(tab)[np.arange(H)[:, None], runs(n1, H)])))
    w2q = unpack_weight(w2_words, w2_scales)
    a = w2q.T @ mxq(z, 0, "e4m3")
    z2 = f64(gn) * (y * (f64(tab2)[np.arange(H)[:, None], runs(n3, H)]) - (0.5 * (y[np.arange(H)[:, None], runs(n4, H)])))
    b = w2q.T @ mxq(z2, 0, "e4m3")
    out_0 = np.maximum(a[np.arange(H)[:, None], runs(n5, H)] + b[np.arange(H)[:, None], runs(n7, H)], a[np.arange(H)[:, None], runs(n6, H)] + b[np.arange(H)[:, None], runs(n8, H)])
    return (out_0,) + planes(out_0)

@@ -1,0 +1,213 @@
+from contextlib import ExitStack
+
+import concourse.mybir as mybir
+
+F32 = mybir.dt.float32
+BF16 = mybir.dt.bfloat16
+I32 = mybir.dt.int32
+U32 = mybir.dt.uint32
+U16 = mybir.dt.uint16
+U8 = mybir.dt.uint8
+FP8X4 = mybir.dt.float8_e4m3fn_x4
+ALU = mybir.AluOpType
+ACT = mybir.ActivationFunctionType
+
+P = 128
+PACK = 4
+T = 2048
+S = 512
+WIDE = 2 * S
+CHUNKS = ((0, 256), (256, 384), (384, 512))
+FLOPS = 3 * 2 * 512 * 512 * 512
+
+
+def words_of(ap):
+    return ap[0].rearrange("p n r -> p (n r)").bitcast(I32)
+
+
+def load_scale_rows(engines, plane, scales):
+    for q in range(4):
+        engines[q].dma_start(plane[32 * q : 32 * q + 4, :].bitcast(I32), scales[0, 4 * q : 4 * q + 4, :].bitcast(I32))
+
+
+def tile_picked_tiepathbkinddkindg_none_po_kernel(
+    tc, x_words, x_scales, w1_words, w1_scales, tab, tab2, gn, w2_words, w2_scales,
+    offs, n1, n2, n3, n4, n5, n6, n7, n8, out_0, out_1, out_2,
+):
+    nc = tc.nc
+    with ExitStack() as ctx:
+        keep = ctx.enter_context(tc.tile_pool(name="keep", bufs=1))
+        shared = ctx.enter_context(tc.tile_pool(name="shared", bufs=1))
+        psum = ctx.enter_context(tc.psum_pool(name="psum", bufs=1))
+
+        def sb(name, shape, dtype, tag=None):
+            return keep.tile(shape, dtype, name=name, tag=tag or name, align_bytes=64)
+
+        def load_list(name, ap):
+            lst = sb(name, [P, S // 16], U16)
+            nc.sync.dma_start(lst[:], ap)
+            return lst
+
+        xs = sb("xs", [P, T], U8)
+        w1s = sb("w1s", [P, S], U8)
+        w2s = sb("w2s", [P, S], U8)
+        gain = sb("gain", [P, PACK], F32)
+        nc.vector.memset(xs[:].bitcast(I32), 0)
+        nc.gpsimd.memset(w1s[:].bitcast(I32), 0)
+        nc.gpsimd.memset(w2s[:].bitcast(I32), 0)
+        l_offs = load_list("offs_l", offs)
+        w1w = sb("w1w", [P, S], I32)
+        nc.sync.dma_start(w1w[:], words_of(w1_words))
+        load_scale_rows([nc.sync] * 4, xs, x_scales)
+        nc.gpsimd.dma_start(gain[:], gn.rearrange("(p t) o -> p (t o)", t=PACK))
+        xw = shared.tile([P, T], I32, name="xw", align_bytes=64, offset=0)
+        nc.sync.dma_start(xw[:], words_of(x_words))
+        load_scale_rows([nc.sync] * 4, w1s, w1_scales)
+
+        tab_rows = tab.rearrange("(p t) j -> p t j", t=PACK)
+        tab2_rows = tab2.rearrange("(p t) j -> p t j", t=PACK)
+        tab_w = [sb("tab_w%d" % t, [P, WIDE], F32) for t in range(PACK)]
+        tab2_w = [sb("tab2_w%d" % t, [P, WIDE], F32) for t in range(PACK)]
+        y_w = [sb("y_w%d" % t, [P, WIDE], F32) for t in range(PACK)]
+        a_w = [sb("a_w%d" % t, [P, WIDE], F32) for t in range(PACK)]
+        b_w = [sb("b_w%d" % t, [P, S], F32) for t in range(PACK)]
+        l1 = load_list("n1_l", n1)
+        nc.sync.dma_start(tab_w[0][:, :S], tab_rows[:, 0, :])
+        w2w = sb("w2w", [P, S], I32)
+        nc.sync.dma_start(w2w[:], words_of(w2_words))
+        load_scale_rows([nc.sync] * 4, w2s, w2_scales)
+        nc.sync.dma_start(tab_w[1][:, :S], tab_rows[:, 1, :])
+        l2 = load_list("n2_l", n2)
+        nc.sync.dma_start(tab_w[2][:, :S], tab_rows[:, 2, :])
+        nc.sync.dma_start(tab_w[3][:, :S], tab_rows[:, 3, :])
+        l3 = load_list("n3_l", n3)
+        l4 = load_list("n4_l", n4)
+        for t in range(PACK):
+            nc.sync.dma_start(tab2_w[t][:, :S], tab2_rows[:, t, :])
+        l5 = load_list("n5_l", n5)
+        l6 = load_list("n6_l", n6)
+        l7 = load_list("n7_l", n7)
+        l8 = load_list("n8_l", n8)
+        for t in range(PACK):
+            nc.vector.memset(tab_w[t][:, S:], 0.0)
+
+        half_gain = sb("half_gain", [P, PACK], F32)
+        nc.scalar.activation(half_gain[:], gain[:], ACT.Copy, scale=-0.5)
+
+        def deal(dealt, raw):
+            nc.vector.tensor_copy(dealt[:].rearrange("p t m -> p m t"), raw[:].rearrange("p (m t) -> p m t", t=PACK))
+            return dealt
+
+        def product(banks, weights, codes, scales):
+            dw, ds = weights
+            for t in range(PACK):
+                nc.tensor.matmul_mx(
+                    banks[t][:], lhsT=dw[:, t, :].bitcast(FP8X4), lhsT_scale=ds[:, t, :],
+                    rhs=codes[:].bitcast(FP8X4), rhs_scale=scales[:], start=True, stop=True,
+                )
+
+        xgs = sb("xgs", [P, S], U8)
+        xgw = sb("xgw", [P, S], I32)
+        nc.vector.tensor_copy(xgs[:], xs[:].indirect(l_offs[:]))
+        w1_dw = deal(sb("w1_dw", [P, PACK, P], I32), w1w)
+        nc.vector.tensor_copy(xgw[:].bitcast(U32), xw[:].bitcast(U32).indirect(l_offs[:]))
+        w1d = (w1_dw, deal(shared.tile([P, PACK, P], U8, name="w1_ds", align_bytes=64, offset=5 * S), w1s))
+        w2d = (
+            deal(shared.tile([P, PACK, P], I32, name="w2_dw", align_bytes=64, offset=0), w2w),
+            deal(shared.tile([P, PACK, P], U8, name="w2_ds", align_bytes=64, offset=4 * S), w2s),
+        )
+
+        y_ps = [psum.tile([P, S], F32, name="y_ps%d" % t, tag="low%d" % t) for t in range(PACK)]
+        product(y_ps, w1d, xgw, xgs)
+        for t in range(PACK):
+            nc.scalar.copy(tab2_w[t][:, S:], y_ps[t][:])
+            nc.scalar.copy(y_w[t][:, :S], y_ps[t][:])
+        for t in range(PACK):
+            nc.scalar.activation(a_w[t][:, S:], y_ps[t][:], ACT.Copy, scale=2.0)
+
+        u = sb("u", [P, PACK, S], F32)
+        for pair in ((0, 1), (2, 3)):
+            for t in pair:
+                nc.vector.tensor_tensor(y_w[t ^ 1][:, S:], tab_w[t][:].indirect(l1[:]), tab2_w[t][:, S:], ALU.subtract)
+            for t in pair:
+                nc.vector.tensor_tensor(u[:, t, :], y_w[t][:].indirect(l2[:]), y_w[t ^ 1][:, S:], ALU.add)
+
+        def quantise(name, values, width, tag):
+            woven = sb(name + "_bf", [P, width, PACK], BF16, tag=tag)
+            nc.scalar.copy(woven[:], values.rearrange("p t n -> p n t"))
+            return woven[:].rearrange("p n t -> p (n t)")
+
+        size = sb("size", [P, PACK, S], F32)
+        z = sb("z", [P, PACK, S], F32)
+        for t in range(PACK):
+            nc.scalar.activation(size[:, t, :], u[:, t, :], ACT.Abs)
+            nc.scalar.activation(z[:, t, :], size[:, t, :], ACT.Copy, scale=gain[:, t : t + 1])
+        z_bf = quantise("z", z[:], S, "hold_z")
+
+        prod = sb("prod", [P, PACK, S], F32)
+        z2 = sb("z2", [P, PACK, S], F32)
+
+        def by_n3(t):
+            nc.vector.tensor_tensor(prod[:, t, :], tab2_w[t][:].indirect(l3[:]), a_w[t][:, S:], ALU.mult)
+
+        def by_n4(t, dst):
+            nc.vector.tensor_tensor(dst, y_w[t][:].indirect(l4[:]), prod[:, t, :], ALU.subtract)
+            nc.scalar.activation(z2[:, t, :], dst, ACT.Copy, scale=half_gain[:, t : t + 1])
+
+        q_lo = sb("q_lo", [P, 2, S], F32)
+        by_n3(0)
+        by_n3(1)
+        by_n4(0, q_lo[:, 0, :])
+        by_n4(1, q_lo[:, 1, :])
+        by_n3(2)
+        by_n3(3)
+        zw = sb("zw", [P, S], U32)
+        zs = sb("zs", [P, S], U8)
+        nc.vector.quantize_mx(zw[:].bitcast(FP8X4), zs[:], z_bf)
+        a_ps = [psum.tile([P, S], F32, name="a_ps%d" % t, tag="high%d" % t) for t in range(PACK)]
+        product(a_ps, w2d, zw, zs)
+        for t in range(PACK):
+            nc.scalar.copy(a_w[t][:, :S], a_ps[t][:])
+        q_hi = sb("q_hi", [P, 2, S], F32, tag="hold_z")
+        by_n4(2, q_hi[:, 0, :])
+        by_n4(3, q_hi[:, 1, :])
+        z2_bf = quantise("z2", z2[:], S, "hold_z2")
+
+        a5 = sb("a5", [P, PACK, S], F32)
+        a6_lo = sb("a6_lo", [P, 2, S], F32)
+        for t in range(PACK):
+            nc.vector.tensor_copy(a5[:, t, :], a_w[t][:].indirect(l5[:]))
+            if t < 2:
+                nc.vector.tensor_copy(a6_lo[:, t, :], a_w[t][:].indirect(l6[:]))
+        z2w = sb("z2w", [P, S], U32)
+        z2s = sb("z2s", [P, S], U8)
+        nc.vector.quantize_mx(z2w[:].bitcast(FP8X4), z2s[:], z2_bf)
+        b_ps = [psum.tile([P, S], F32, name="b_ps%d" % t, tag="low%d" % t) for t in range(PACK)]
+        product(b_ps, w2d, z2w, z2s)
+        for t in range(PACK):
+            nc.scalar.copy(b_w[t][:], b_ps[t][:])
+        a6_hi = sb("a6_hi", [P, 2, S], F32, tag="hold_z2")
+        for t in (2, 3):
+            nc.vector.tensor_copy(a6_hi[:, t - 2, :], a_w[t][:].indirect(l6[:]))
+        a6 = [a6_lo[:, 0, :], a6_lo[:, 1, :], a6_hi[:, 0, :], a6_hi[:, 1, :]]
+
+        ow = sb("ow", [P, S], U32)
+        osc = sb("osc", [P, S], U8)
+        out_rows = out_0.rearrange("(p t) j -> p t j", t=PACK)
+        out_words = words_of(out_1)
+        for c, (lo, hi) in enumerate(CHUNKS):
+            n = hi - lo
+            s1 = sb("s1_%d" % c, [P, PACK, n], F32, tag="hold_o" if c == 2 else None)
+            s2 = sb("s2_%d" % c, [P, PACK, n], F32)
+            for t in range(PACK):
+                nc.vector.tensor_tensor(s1[:, t, :], b_w[t][:].indirect(l7[:, lo // 16 : hi // 16]), a5[:, t, lo:hi], ALU.add)
+                nc.vector.tensor_tensor(s2[:, t, :], b_w[t][:].indirect(l8[:, lo // 16 : hi // 16]), a6[t][:, lo:hi], ALU.add)
+            res = sb("res%d" % c, [P, PACK, n], F32)
+            nc.vector.tensor_tensor(res[:], s1[:], s2[:], ALU.max)
+            nc.sync.dma_start(out_rows[:, :, lo:hi], res[:])
+            o_bf = quantise("o%d" % c, res[:], n, "hold_o" if c == 0 else None)
+            nc.vector.quantize_mx(ow[:, lo:hi].bitcast(FP8X4), osc[:, lo:hi], o_bf)
+            nc.sync.dma_start(out_words[:, lo:hi], ow[:, lo:hi].bitcast(I32))
+        for q in range(4):
+            eng = nc.scalar if q % 2 else nc.sync
+            eng.dma_start(out_2[0, 4 * q : 4 * q + 4, :].bitcast(I32), osc[32 * q : 32 * q + 4, :].bitcast(I32))

@@ -59,7 +59,6 @@ def tile_picked_tiepathbkinddkindg_none_po_kernel(
         w1w = sb("w1w", [P, S], I32)
         nc.sync.dma_start(w1w[:], words_of(w1_words))
         load_scale_rows([nc.sync] * 4, xs, x_scales)
-        nc.gpsimd.dma_start(gain[:], gn.rearrange("(p t) o -> p (t o)", t=PACK))
         xw = shared.tile([P, T], I32, name="xw", align_bytes=64, offset=0)
         nc.sync.dma_start(xw[:], words_of(x_words))
         load_scale_rows([nc.sync] * 4, w1s, w1_scales)
@@ -80,6 +79,7 @@ def tile_picked_tiepathbkinddkindg_none_po_kernel(
         l2 = load_list("n2_l", n2)
         nc.sync.dma_start(tab_w[2][:, :S], tab_rows[:, 2, :])
         nc.sync.dma_start(tab_w[3][:, :S], tab_rows[:, 3, :])
+        nc.sync.dma_start(gain[:], gn.rearrange("(p t) o -> p (t o)", t=PACK))
         l3 = load_list("n3_l", n3)
         l4 = load_list("n4_l", n4)
         for t in range(PACK):
@@ -89,13 +89,15 @@ def tile_picked_tiepathbkinddkindg_none_po_kernel(
         l7 = load_list("n7_l", n7)
         l8 = load_list("n8_l", n8)
         for t in range(PACK):
-            nc.vector.memset(tab_w[t][:, S:], 0.0)
+            nc.gpsimd.memset(tab_w[t][:, S:], 0.0)
 
         half_gain = sb("half_gain", [P, PACK], F32)
         nc.scalar.activation(half_gain[:], gain[:], ACT.Copy, scale=-0.5)
 
-        def deal(dealt, raw):
-            nc.vector.tensor_copy(dealt[:].rearrange("p t m -> p m t"), raw[:].rearrange("p (m t) -> p m t", t=PACK))
+        def deal(dealt, raw, run):
+            nc.vector.tensor_copy(
+                dealt[:].rearrange("p t (c i) -> p c t i", i=run), raw[:].rearrange("p (c i t) -> p c t i", i=run, t=PACK)
+            )
             return dealt
 
         def product(banks, weights, codes, scales):
@@ -107,34 +109,49 @@ def tile_picked_tiepathbkinddkindg_none_po_kernel(
                 )
 
         xgs = sb("xgs", [P, S], U8)
-        xgw = sb("xgw", [P, S], I32)
         nc.vector.tensor_copy(xgs[:], xs[:].indirect(l_offs[:]))
-        w1_dw = deal(sb("w1_dw", [P, PACK, P], I32), w1w)
-        nc.vector.tensor_copy(xgw[:].bitcast(U32), xw[:].bitcast(U32).indirect(l_offs[:]))
-        w1d = (w1_dw, deal(shared.tile([P, PACK, P], U8, name="w1_ds", align_bytes=64, offset=5 * S), w1s))
+        w1_dw = deal(sb("w1_dw", [P, PACK, P], I32), w1w, 4)
+        H = S // 2
+        xg0 = sb("xg0", [P, H], I32)
+        nc.vector.tensor_copy(xg0[:].bitcast(U32), xw[:].bitcast(U32).indirect(l_offs[:, : H // 16]))
+        w1_ds = deal(sb("w1_ds", [P, PACK, P], U8), w1s, 16)
+        xg1 = sb("xg1", [P, H], I32, tag="w1s")
+        nc.vector.tensor_copy(xg1[:].bitcast(U32), xw[:].bitcast(U32).indirect(l_offs[:, H // 16 :]))
         w2d = (
-            deal(shared.tile([P, PACK, P], I32, name="w2_dw", align_bytes=64, offset=0), w2w),
-            deal(shared.tile([P, PACK, P], U8, name="w2_ds", align_bytes=64, offset=4 * S), w2s),
+            deal(shared.tile([P, PACK, P], I32, name="w2_dw", align_bytes=64, offset=0), w2w, 4),
+            deal(shared.tile([P, PACK, P], U8, name="w2_ds", align_bytes=64, offset=4 * S), w2s, 16),
         )
 
-        y_ps = [psum.tile([P, S], F32, name="y_ps%d" % t, tag="low%d" % t) for t in range(PACK)]
-        product(y_ps, w1d, xgw, xgs)
+        y_ps = [[psum.tile([P, H], F32, name="y_ps%d%d" % (t, h), tag=("low%d", "high%d")[h] % t) for h in range(2)] for t in range(PACK)]
+        for pair in ((0, 1), (2, 3)):
+            for h, xg in enumerate((xg0, xg1)):
+                for t in pair:
+                    nc.tensor.matmul_mx(
+                        y_ps[t][h][:], lhsT=w1_dw[:, t, :].bitcast(FP8X4), lhsT_scale=w1_ds[:, t, :],
+                        rhs=xg[:].bitcast(FP8X4), rhs_scale=xgs[:, h * H : (h + 1) * H], start=True, stop=True,
+                    )
+                    nc.scalar.copy(tab2_w[t][:, S + h * H : S + (h + 1) * H], y_ps[t][h][:])
+            for t in pair:
+                for h in range(2):
+                    nc.scalar.copy(y_w[t][:, h * H : (h + 1) * H], y_ps[t][h][:])
         for t in range(PACK):
-            nc.scalar.copy(tab2_w[t][:, S:], y_ps[t][:])
-            nc.scalar.copy(y_w[t][:, :S], y_ps[t][:])
-        for t in range(PACK):
-            nc.scalar.activation(a_w[t][:, S:], y_ps[t][:], ACT.Copy, scale=2.0)
+            for h in range(2):
+                nc.scalar.activation(a_w[t][:, S + h * H : S + (h + 1) * H], y_ps[t][h][:], ACT.Copy, scale=2.0)
 
         u = sb("u", [P, PACK, S], F32)
         for pair in ((0, 1), (2, 3)):
-            for t in pair:
-                nc.vector.tensor_tensor(y_w[t ^ 1][:, S:], tab_w[t][:].indirect(l1[:]), tab2_w[t][:, S:], ALU.subtract)
+            for lo, hi in ((0, H), (H, S)) if pair[0] == 0 else ((0, S),):
+                for t in pair:
+                    nc.vector.tensor_tensor(
+                        y_w[t ^ 1][:, S + lo : S + hi], tab_w[t][:].indirect(l1[:, lo // 16 : hi // 16]),
+                        tab2_w[t][:, S + lo : S + hi], ALU.subtract,
+                    )
             for t in pair:
                 nc.vector.tensor_tensor(u[:, t, :], y_w[t][:].indirect(l2[:]), y_w[t ^ 1][:, S:], ALU.add)
 
         def quantise(name, values, width, tag):
             woven = sb(name + "_bf", [P, width, PACK], BF16, tag=tag)
-            nc.scalar.copy(woven[:], values.rearrange("p t n -> p n t"))
+            nc.scalar.copy(woven[:].rearrange("p (c i) t -> p c t i", i=4), values.rearrange("p t (c i) -> p c t i", i=4))
             return woven[:].rearrange("p n t -> p (n t)")
 
         size = sb("size", [P, PACK, S], F32)
@@ -203,9 +220,17 @@ def tile_picked_tiepathbkinddkindg_none_po_kernel(
                 nc.vector.tensor_tensor(s1[:, t, :], b_w[t][:].indirect(l7[:, lo // 16 : hi // 16]), a5[:, t, lo:hi], ALU.add)
                 nc.vector.tensor_tensor(s2[:, t, :], b_w[t][:].indirect(l8[:, lo // 16 : hi // 16]), a6[t][:, lo:hi], ALU.add)
             res = sb("res%d" % c, [P, PACK, n], F32)
+            if c == 2:
+                woven = sb("o_last", [P, n, PACK], BF16)
+                nc.vector.tensor_tensor(
+                    woven[:].rearrange("p (c i) t -> p c t i", i=4), s1[:].rearrange("p t (c i) -> p c t i", i=4),
+                    s2[:].rearrange("p t (c i) -> p c t i", i=4), ALU.max,
+                )
+                o_bf = woven[:].rearrange("p n t -> p (n t)")
             nc.vector.tensor_tensor(res[:], s1[:], s2[:], ALU.max)
-            nc.sync.dma_start(out_rows[:, :, lo:hi], res[:])
-            o_bf = quantise("o%d" % c, res[:], n, "hold_o" if c == 0 else None)
+            (nc.scalar if c == 2 else nc.sync).dma_start(out_rows[:, :, lo:hi], res[:])
+            if c < 2:
+                o_bf = quantise("o%d" % c, res[:], n, "hold_o" if c == 0 else None)
             nc.vector.quantize_mx(ow[:, lo:hi].bitcast(FP8X4), osc[:, lo:hi], o_bf)
             nc.sync.dma_start(out_words[:, lo:hi], ow[:, lo:hi].bitcast(I32))
         for q in range(4):

@@ -151,7 +151,7 @@ def tile_picked_tiepathbkinddkindg_none_po_kernel(
 
         def quantise(name, values, width, tag):
             woven = sb(name + "_bf", [P, width, PACK], BF16, tag=tag)
-            nc.scalar.copy(woven[:].rearrange("p (c i) t -> p c t i", i=4), values.rearrange("p t (c i) -> p c t i", i=4))
+            nc.scalar.copy(woven[:], values.rearrange("p t n -> p n t"))
             return woven[:].rearrange("p n t -> p (n t)")
 
         size = sb("size", [P, PACK, S], F32)
@@ -216,18 +216,19 @@ def tile_picked_tiepathbkinddkindg_none_po_kernel(
             n = hi - lo
             s1 = sb("s1_%d" % c, [P, PACK, n], F32, tag="hold_o" if c == 2 else None)
             s2 = sb("s2_%d" % c, [P, PACK, n], F32)
+            res = sb("res%d" % c, [P, PACK, n], F32)
             for t in range(PACK):
+                if c == 2 and t == 3:
+                    nc.vector.tensor_tensor(res[:, :3, :], s1[:, :3, :], s2[:, :3, :], ALU.max)
                 nc.vector.tensor_tensor(s1[:, t, :], b_w[t][:].indirect(l7[:, lo // 16 : hi // 16]), a5[:, t, lo:hi], ALU.add)
                 nc.vector.tensor_tensor(s2[:, t, :], b_w[t][:].indirect(l8[:, lo // 16 : hi // 16]), a6[t][:, lo:hi], ALU.add)
-            res = sb("res%d" % c, [P, PACK, n], F32)
             if c == 2:
+                nc.vector.tensor_tensor(res[:, 3, :], s1[:, 3, :], s2[:, 3, :], ALU.max)
                 woven = sb("o_last", [P, n, PACK], BF16)
-                nc.vector.tensor_tensor(
-                    woven[:].rearrange("p (c i) t -> p c t i", i=4), s1[:].rearrange("p t (c i) -> p c t i", i=4),
-                    s2[:].rearrange("p t (c i) -> p c t i", i=4), ALU.max,
-                )
+                nc.vector.tensor_copy(woven[:], res[:].rearrange("p t n -> p n t"))
                 o_bf = woven[:].rearrange("p n t -> p (n t)")
-            nc.vector.tensor_tensor(res[:], s1[:], s2[:], ALU.max)
+            else:
+                nc.vector.tensor_tensor(res[:], s1[:], s2[:], ALU.max)
             (nc.scalar if c == 2 else nc.sync).dma_start(out_rows[:, :, lo:hi], res[:])
             if c < 2:
                 o_bf = quantise("o%d" % c, res[:], n, "hold_o" if c == 0 else None)

@@ -53,8 +53,8 @@ def tile_picked_tiepathbkinddkindg_none_po_kernel(
         w2s = sb("w2s", [P, S], U8)
         gain = sb("gain", [P, PACK], F32)
         nc.vector.memset(xs[:].bitcast(I32), 0)
-        nc.gpsimd.memset(w1s[:].bitcast(I32), 0)
-        nc.gpsimd.memset(w2s[:].bitcast(I32), 0)
+        nc.vector.memset(w1s[:].bitcast(I32), 0)
+        nc.vector.memset(w2s[:].bitcast(I32), 0)
         l_offs = load_list("offs_l", offs)
         w1w = sb("w1w", [P, S], I32)
         nc.sync.dma_start(w1w[:], words_of(w1_words))
@@ -89,7 +89,7 @@ def tile_picked_tiepathbkinddkindg_none_po_kernel(
         l7 = load_list("n7_l", n7)
         l8 = load_list("n8_l", n8)
         for t in range(PACK):
-            nc.gpsimd.memset(tab_w[t][:, S:], 0.0)
+            nc.vector.memset(tab_w[t][:, S:], 0.0)
 
         half_gain = sb("half_gain", [P, PACK], F32)
         nc.scalar.activation(half_gain[:], gain[:], ACT.Copy, scale=-0.5)
@@ -151,7 +151,7 @@ def tile_picked_tiepathbkinddkindg_none_po_kernel(
 
         def quantise(name, values, width, tag):
             woven = sb(name + "_bf", [P, width, PACK], BF16, tag=tag)
-            nc.scalar.copy(woven[:], values.rearrange("p t n -> p n t"))
+            nc.scalar.copy(woven[:].rearrange("p (c i) t -> p c t i", i=4), values.rearrange("p t (c i) -> p c t i", i=4))
             return woven[:].rearrange("p n t -> p (n t)")
 
         size = sb("size", [P, PACK, S], F32)
@@ -162,7 +162,7 @@ def tile_picked_tiepathbkinddkindg_none_po_kernel(
         z_bf = quantise("z", z[:], S, "hold_z")
 
         prod = sb("prod", [P, PACK, S], F32)
-        z2 = sb("z2", [P, PACK, S], F32)
+        z2 = sb("z2", [P, PACK, S], F32, tag="z")
 
         def by_n3(t):
             nc.vector.tensor_tensor(prod[:, t, :], tab2_w[t][:].indirect(l3[:]), a_w[t][:, S:], ALU.mult)
@@ -214,24 +214,16 @@ def tile_picked_tiepathbkinddkindg_none_po_kernel(
         out_words = words_of(out_1)
         for c, (lo, hi) in enumerate(CHUNKS):
             n = hi - lo
-            s1 = sb("s1_%d" % c, [P, PACK, n], F32, tag="hold_o" if c == 2 else None)
-            s2 = sb("s2_%d" % c, [P, PACK, n], F32)
             res = sb("res%d" % c, [P, PACK, n], F32)
-            for t in range(PACK):
-                if c == 2 and t == 3:
-                    nc.vector.tensor_tensor(res[:, :3, :], s1[:, :3, :], s2[:, :3, :], ALU.max)
-                nc.vector.tensor_tensor(s1[:, t, :], b_w[t][:].indirect(l7[:, lo // 16 : hi // 16]), a5[:, t, lo:hi], ALU.add)
-                nc.vector.tensor_tensor(s2[:, t, :], b_w[t][:].indirect(l8[:, lo // 16 : hi // 16]), a6[t][:, lo:hi], ALU.add)
-            if c == 2:
-                nc.vector.tensor_tensor(res[:, 3, :], s1[:, 3, :], s2[:, 3, :], ALU.max)
-                woven = sb("o_last", [P, n, PACK], BF16)
-                nc.vector.tensor_copy(woven[:], res[:].rearrange("p t n -> p n t"))
-                o_bf = woven[:].rearrange("p n t -> p (n t)")
-            else:
-                nc.vector.tensor_tensor(res[:], s1[:], s2[:], ALU.max)
-            (nc.scalar if c == 2 else nc.sync).dma_start(out_rows[:, :, lo:hi], res[:])
-            if c < 2:
-                o_bf = quantise("o%d" % c, res[:], n, "hold_o" if c == 0 else None)
+            groups = ((0, 2), (2, 3), (3, 4)) if c == 2 else ((0, 4),)
+            for t0, t1 in groups:
+                sums = sb("sums%d_%d" % (c, t0), [P, 2, t1 - t0, n], F32, tag="hold_o" if t0 == 2 else None)
+                for t in range(t0, t1):
+                    nc.vector.tensor_tensor(sums[:, 0, t - t0, :], b_w[t][:].indirect(l7[:, lo // 16 : hi // 16]), a5[:, t, lo:hi], ALU.add)
+                    nc.vector.tensor_tensor(sums[:, 1, t - t0, :], b_w[t][:].indirect(l8[:, lo // 16 : hi // 16]), a6[t][:, lo:hi], ALU.add)
+                nc.vector.tensor_tensor(res[:, t0:t1, :], sums[:, 0, :, :], sums[:, 1, :, :], ALU.max)
+            nc.sync.dma_start(out_rows[:, :, lo:hi], res[:])
+            o_bf = quantise("o%d" % c, res[:], n, "hold_o" if c == 0 else None)
             nc.vector.quantize_mx(ow[:, lo:hi].bitcast(FP8X4), osc[:, lo:hi], o_bf)
             nc.sync.dma_start(out_words[:, lo:hi], ow[:, lo:hi].bitcast(I32))
         for q in range(4):

from contextlib import ExitStack

import concourse.mybir as mybir

F32 = mybir.dt.float32
BF16 = mybir.dt.bfloat16
I32 = mybir.dt.int32
U32 = mybir.dt.uint32
U16 = mybir.dt.uint16
U8 = mybir.dt.uint8
FP8X4 = mybir.dt.float8_e4m3fn_x4
ALU = mybir.AluOpType
ACT = mybir.ActivationFunctionType

P = 128
PACK = 4
T = 2048
S = 512
WIDE = 2 * S
CHUNKS = ((0, 256), (256, 384), (384, 512))
FLOPS = 3 * 2 * 512 * 512 * 512


def words_of(ap):
    return ap[0].rearrange("p n r -> p (n r)").bitcast(I32)


def load_scale_rows(engines, plane, scales):
    for q in range(4):
        engines[q].dma_start(plane[32 * q : 32 * q + 4, :].bitcast(I32), scales[0, 4 * q : 4 * q + 4, :].bitcast(I32))


def tile_picked_tiepathbkinddkindg_none_po_kernel(
    tc, x_words, x_scales, w1_words, w1_scales, tab, tab2, gn, w2_words, w2_scales,
    offs, n1, n2, n3, n4, n5, n6, n7, n8, out_0, out_1, out_2,
):
    nc = tc.nc
    with ExitStack() as ctx:
        keep = ctx.enter_context(tc.tile_pool(name="keep", bufs=1))
        shared = ctx.enter_context(tc.tile_pool(name="shared", bufs=1))
        psum = ctx.enter_context(tc.psum_pool(name="psum", bufs=1))

        def sb(name, shape, dtype, tag=None):
            return keep.tile(shape, dtype, name=name, tag=tag or name, align_bytes=64)

        def load_list(name, ap):
            lst = sb(name, [P, S // 16], U16)
            nc.sync.dma_start(lst[:], ap)
            return lst

        xs = sb("xs", [P, T], U8)
        w1s = sb("w1s", [P, S], U8)
        w2s = sb("w2s", [P, S], U8)
        gain = sb("gain", [P, PACK], F32)
        nc.vector.memset(xs[:].bitcast(I32), 0)
        nc.vector.memset(w1s[:].bitcast(I32), 0)
        nc.vector.memset(w2s[:].bitcast(I32), 0)
        l_offs = load_list("offs_l", offs)
        w1w = sb("w1w", [P, S], I32)
        nc.sync.dma_start(w1w[:], words_of(w1_words))
        load_scale_rows([nc.sync] * 4, xs, x_scales)
        xw = shared.tile([P, T], I32, name="xw", align_bytes=64, offset=0)
        nc.sync.dma_start(xw[:], words_of(x_words))
        load_scale_rows([nc.sync] * 4, w1s, w1_scales)

        tab_rows = tab.rearrange("(p t) j -> p t j", t=PACK)
        tab2_rows = tab2.rearrange("(p t) j -> p t j", t=PACK)
        tab_w = [sb("tab_w%d" % t, [P, WIDE], F32) for t in range(PACK)]
        tab2_w = [sb("tab2_w%d" % t, [P, WIDE], F32) for t in range(PACK)]
        y_w = [sb("y_w%d" % t, [P, WIDE], F32) for t in range(PACK)]
        a_w = [sb("a_w%d" % t, [P, WIDE], F32) for t in range(PACK)]
        b_w = [sb("b_w%d" % t, [P, S], F32) for t in range(PACK)]
        l1 = load_list("n1_l", n1)
        nc.sync.dma_start(tab_w[0][:, :S], tab_rows[:, 0, :])
        w2w = sb("w2w", [P, S], I32)
        nc.sync.dma_start(w2w[:], words_of(w2_words))
        load_scale_rows([nc.sync] * 4, w2s, w2_scales)
        nc.sync.dma_start(tab_w[1][:, :S], tab_rows[:, 1, :])
        l2 = load_list("n2_l", n2)
        nc.sync.dma_start(tab_w[2][:, :S], tab_rows[:, 2, :])
        nc.sync.dma_start(tab_w[3][:, :S], tab_rows[:, 3, :])
        nc.sync.dma_start(gain[:], gn.rearrange("(p t) o -> p (t o)", t=PACK))
        l3 = load_list("n3_l", n3)
        l4 = load_list("n4_l", n4)
        for t in range(PACK):
            nc.sync.dma_start(tab2_w[t][:, :S], tab2_rows[:, t, :])
        l5 = load_list("n5_l", n5)
        l6 = load_list("n6_l", n6)
        l7 = load_list("n7_l", n7)
        l8 = load_list("n8_l", n8)
        for t in range(PACK):
            nc.vector.memset(tab_w[t][:, S:], 0.0)

        half_gain = sb("half_gain", [P, PACK], F32)
        nc.scalar.activation(half_gain[:], gain[:], ACT.Copy, scale=-0.5)

        def deal(dealt, raw, run):
            nc.vector.tensor_copy(
                dealt[:].rearrange("p t (c i) -> p c t i", i=run), raw[:].rearrange("p (c i t) -> p c t i", i=run, t=PACK)
            )
            return dealt

        def product(banks, weights, codes, scales):
            dw, ds = weights
            for t in range(PACK):
                nc.tensor.matmul_mx(
                    banks[t][:], lhsT=dw[:, t, :].bitcast(FP8X4), lhsT_scale=ds[:, t, :],
                    rhs=codes[:].bitcast(FP8X4), rhs_scale=scales[:], start=True, stop=True,
                )

        xgs = sb("xgs", [P, S], U8)
        nc.vector.tensor_copy(xgs[:], xs[:].indirect(l_offs[:]))
        w1_dw = deal(sb("w1_dw", [P, PACK, P], I32), w1w, 4)
        H = S // 2
        xg0 = sb("xg0", [P, H], I32)
        nc.vector.tensor_copy(xg0[:].bitcast(U32), xw[:].bitcast(U32).indirect(l_offs[:, : H // 16]))
        w1_ds = deal(sb("w1_ds", [P, PACK, P], U8), w1s, 16)
        xg1 = sb("xg1", [P, H], I32, tag="w1s")
        nc.vector.tensor_copy(xg1[:].bitcast(U32), xw[:].bitcast(U32).indirect(l_offs[:, H // 16 :]))
        w2d = (
            deal(shared.tile([P, PACK, P], I32, name="w2_dw", align_bytes=64, offset=0), w2w, 4),
            deal(shared.tile([P, PACK, P], U8, name="w2_ds", align_bytes=64, offset=4 * S), w2s, 16),
        )

        y_ps = [[psum.tile([P, H], F32, name="y_ps%d%d" % (t, h), tag=("low%d", "high%d")[h] % t) for h in range(2)] for t in range(PACK)]
        for pair in ((0, 1), (2, 3)):
            for h, xg in enumerate((xg0, xg1)):
                for t in pair:
                    nc.tensor.matmul_mx(
                        y_ps[t][h][:], lhsT=w1_dw[:, t, :].bitcast(FP8X4), lhsT_scale=w1_ds[:, t, :],
                        rhs=xg[:].bitcast(FP8X4), rhs_scale=xgs[:, h * H : (h + 1) * H], start=True, stop=True,
                    )
                    nc.scalar.copy(tab2_w[t][:, S + h * H : S + (h + 1) * H], y_ps[t][h][:])
            for t in pair:
                for h in range(2):
                    nc.scalar.copy(y_w[t][:, h * H : (h + 1) * H], y_ps[t][h][:])
        for t in range(PACK):
            for h in range(2):
                nc.scalar.activation(a_w[t][:, S + h * H : S + (h + 1) * H], y_ps[t][h][:], ACT.Copy, scale=2.0)

        u = sb("u", [P, PACK, S], F32)
        for pair in ((0, 1), (2, 3)):
            for lo, hi in ((0, H), (H, S)) if pair[0] == 0 else ((0, S),):
                for t in pair:
                    nc.vector.tensor_tensor(
                        y_w[t ^ 1][:, S + lo : S + hi], tab_w[t][:].indirect(l1[:, lo // 16 : hi // 16]),
                        tab2_w[t][:, S + lo : S + hi], ALU.subtract,
                    )
            for t in pair:
                nc.vector.tensor_tensor(u[:, t, :], y_w[t][:].indirect(l2[:]), y_w[t ^ 1][:, S:], ALU.add)

        def quantise(name, values, width, tag):
            woven = sb(name + "_bf", [P, width, PACK], BF16, tag=tag)
            nc.scalar.copy(woven[:].rearrange("p (c i) t -> p c t i", i=4), values.rearrange("p t (c i) -> p c t i", i=4))
            return woven[:].rearrange("p n t -> p (n t)")

        size = sb("size", [P, PACK, S], F32)
        z = sb("z", [P, PACK, S], F32)
        for t in range(PACK):
            nc.scalar.activation(size[:, t, :], u[:, t, :], ACT.Abs)
            nc.scalar.activation(z[:, t, :], size[:, t, :], ACT.Copy, scale=gain[:, t : t + 1])
        z_bf = quantise("z", z[:], S, "hold_z")

        prod = sb("prod", [P, PACK, S], F32)
        z2 = sb("z2", [P, PACK, S], F32, tag="z")

        def by_n3(t):
            nc.vector.tensor_tensor(prod[:, t, :], tab2_w[t][:].indirect(l3[:]), a_w[t][:, S:], ALU.mult)

        def by_n4(t, dst):
            nc.vector.tensor_tensor(dst, y_w[t][:].indirect(l4[:]), prod[:, t, :], ALU.subtract)
            nc.scalar.activation(z2[:, t, :], dst, ACT.Copy, scale=half_gain[:, t : t + 1])

        q_lo = sb("q_lo", [P, 2, S], F32)
        by_n3(0)
        by_n3(1)
        by_n4(0, q_lo[:, 0, :])
        by_n4(1, q_lo[:, 1, :])
        by_n3(2)
        by_n3(3)
        zw = sb("zw", [P, S], U32)
        zs = sb("zs", [P, S], U8)
        nc.vector.quantize_mx(zw[:].bitcast(FP8X4), zs[:], z_bf)
        a_ps = [psum.tile([P, S], F32, name="a_ps%d" % t, tag="high%d" % t) for t in range(PACK)]
        product(a_ps, w2d, zw, zs)
        for t in range(PACK):
            nc.scalar.copy(a_w[t][:, :S], a_ps[t][:])
        q_hi = sb("q_hi", [P, 2, S], F32, tag="hold_z")
        by_n4(2, q_hi[:, 0, :])
        by_n4(3, q_hi[:, 1, :])
        z2_bf = quantise("z2", z2[:], S, "hold_z2")

        a5 = sb("a5", [P, PACK, S], F32)
        a6_lo = sb("a6_lo", [P, 2, S], F32)
        for t in range(PACK):
            nc.vector.tensor_copy(a5[:, t, :], a_w[t][:].indirect(l5[:]))
            if t < 2:
                nc.vector.tensor_copy(a6_lo[:, t, :], a_w[t][:].indirect(l6[:]))
        z2w = sb("z2w", [P, S], U32)
        z2s = sb("z2s", [P, S], U8)
        nc.vector.quantize_mx(z2w[:].bitcast(FP8X4), z2s[:], z2_bf)
        b_ps = [psum.tile([P, S], F32, name="b_ps%d" % t, tag="low%d" % t) for t in range(PACK)]
        product(b_ps, w2d, z2w, z2s)
        for t in range(PACK):
            nc.scalar.copy(b_w[t][:], b_ps[t][:])
        a6_hi = sb("a6_hi", [P, 2, S], F32, tag="hold_z2")
        for t in (2, 3):
            nc.vector.tensor_copy(a6_hi[:, t - 2, :], a_w[t][:].indirect(l6[:]))
        a6 = [a6_lo[:, 0, :], a6_lo[:, 1, :], a6_hi[:, 0, :], a6_hi[:, 1, :]]

        ow = sb("ow", [P, S], U32)
        osc = sb("osc", [P, S], U8)
        out_rows = out_0.rearrange("(p t) j -> p t j", t=PACK)
        out_words = words_of(out_1)
        for c, (lo, hi) in enumerate(CHUNKS):
            n = hi - lo
            res = sb("res%d" % c, [P, PACK, n], F32)
            groups = ((0, 2), (2, 3), (3, 4)) if c == 2 else ((0, 4),)
            for t0, t1 in groups:
                sums = sb("sums%d_%d" % (c, t0), [P, 2, t1 - t0, n], F32, tag="hold_o" if t0 == 2 else None)
                for t in range(t0, t1):
                    nc.vector.tensor_tensor(sums[:, 0, t - t0, :], b_w[t][:].indirect(l7[:, lo // 16 : hi // 16]), a5[:, t, lo:hi], ALU.add)
                    nc.vector.tensor_tensor(sums[:, 1, t - t0, :], b_w[t][:].indirect(l8[:, lo // 16 : hi // 16]), a6[t][:, lo:hi], ALU.add)
                nc.vector.tensor_tensor(res[:, t0:t1, :], sums[:, 0, :, :], sums[:, 1, :, :], ALU.max)
            nc.sync.dma_start(out_rows[:, :, lo:hi], res[:])
            o_bf = quantise("o%d" % c, res[:], n, "hold_o" if c == 0 else None)
            nc.vector.quantize_mx(ow[:, lo:hi].bitcast(FP8X4), osc[:, lo:hi], o_bf)
            nc.sync.dma_start(out_words[:, lo:hi], ow[:, lo:hi].bitcast(I32))
        for q in range(4):
            eng = nc.scalar if q % 2 else nc.sync
            eng.dma_start(out_2[0, 4 * q : 4 * q + 4, :].bitcast(I32), osc[32 * q : 32 * q + 4, :].bitcast(I32))
